import numpy as np
import ml_dtypes


def mxq(x, axis, fmt="e4m3"):
    dtype, down = {"e4m3": (ml_dtypes.float8_e4m3fn, 7), "e5m2": (ml_dtypes.float8_e5m2, 14)}[fmt]
    v = np.moveaxis(np.asarray(x, np.float32).astype(ml_dtypes.bfloat16).astype(np.float64), axis, -1)
    blocks = v.reshape(v.shape[:-1] + (-1, 32))
    amax = np.abs(blocks).max(-1, keepdims=True)
    byte = np.maximum(np.where(amax > 0, np.frexp(amax)[1] - 1 + 127, 0) - down, 1)
    scale = np.exp2(byte - 127.0)
    codes = (blocks / scale).astype(np.float32).astype(dtype).astype(np.float64)
    return np.moveaxis((codes * scale).reshape(v.shape), -1, axis)


WIDE = False


def mx_kscale(k):
    if not WIDE:
        return np.ones(k)
    levels = np.array([10, -10, 5, -5, 0])
    if k % 512:
        return np.exp2(np.random.permutation(np.resize(levels, k // 32))).repeat(32)
    a = np.empty((k // 512, 16))
    for p in range(k // 512):
        a[p, :8] = np.random.permutation(np.resize(levels, 8))
        for g in range(8):
            far = levels[np.abs(levels - a[p, g]) >= 10]
            a[p, g + 8] = far[np.random.randint(len(far))]
    return np.exp2(a.ravel()).repeat(32)


def f64(x):
    return np.asarray(x).astype(np.float64)


def striped(idx):
    return np.tile(idx.reshape(-1, 16).T, (8, 1)).astype(np.uint16)


def unstriped(offs):
    return offs[:16].T.reshape(-1).astype(np.int64)


K, T, S, V, H, N = 512, 2048, 1024, 512, 512, 256


def setup_inputs():
    n = np.random.standard_normal
    s = mx_kscale(K)[:, None]
    u = mx_kscale(H)
    return {
        "xT": (n((K, T)) * s).astype(np.float32),
        "w1": (n((K, H)) / np.sqrt(K) / s * u).astype(np.float32),
        "w2": (n((H, N)) / np.sqrt(3 * H) / u[:, None]).astype(np.float32),
        "w3": (n((H, N)) / np.sqrt(3 * H) / u[:, None]).astype(np.float32),
        "w4": (n((H, N)) / np.sqrt(3 * H) / u[:, None]).astype(np.float32),
        "offs": striped(np.random.permutation(T)[:S]),
        "pos1": striped(np.random.permutation(S)[:V]),
        "pos2": striped(np.random.permutation(S)[:V]),
        "pos3": striped(np.random.permutation(S)[:V]),
        "pos4": striped(np.random.permutation(S)[:V]),
    }


def reference(xT, w1, w2, w3, w4, offs, pos1, pos2, pos3, pos4):
    xq = mxq(f64(xT)[:, unstriped(offs)], 0, "e4m3")
    h = mxq(f64(w1), 0, "e4m3").T @ xq
    g0 = h[:, unstriped(pos1)]
    g1 = h[:, unstriped(pos2)]
    g2 = h[:, unstriped(pos3)]
    g3 = h[:, unstriped(pos4)]
    z1 = (g0 + g1 + g2 + g3) / 4
    z2 = np.maximum(np.maximum(np.maximum(g0, g1), g2), g3)
    z3 = np.minimum(np.minimum(np.minimum(g0, g1), g2), g3)
    return mxq(f64(w2), 0, "e4m3").T @ mxq(z1, 0, "e4m3") + mxq(f64(w3), 0, "e4m3").T @ mxq(z2, 0, "e4m3") + mxq(f64(w4), 0, "e4m3").T @ mxq(z3, 0, "e4m3")

@@ -1,0 +1,193 @@
+from contextlib import ExitStack
+
+import concourse.mybir as mybir
+from concourse.masks import make_identity
+
+K, T, S, V, H, N = 512, 2048, 1024, 512, 512, 256
+FLOPS = 2 * (K * H * S + 3 * H * N * V)
+
+F32 = mybir.dt.float32
+BF16 = mybir.dt.bfloat16
+U32 = mybir.dt.uint32
+U16 = mybir.dt.uint16
+U8 = mybir.dt.uint8
+FP8X4 = mybir.dt.float8_e4m3fn_x4
+COPY = mybir.ActivationFunctionType.Copy
+MAX = mybir.AluOpType.max
+MIN = mybir.AluOpType.min
+
+P = 128
+D = 4
+CHUNK = 512
+PIECES = (512, 256, 256)
+PARTS = (256, 256)
+
+
+def spans(widths):
+    starts = [sum(widths[:i]) for i in range(len(widths))]
+    return [slice(a, a + w) for a, w in zip(starts, widths)]
+
+
+def tile_picked_pna_none_e_kernel(tc, xT, w1, w2, w3, w4, offs, pos1, pos2, pos3, pos4, out):
+    nc = tc.nc
+    with ExitStack() as ctx:
+        lists = ctx.enter_context(tc.tile_pool(name="lists", bufs=1))
+        sb = ctx.enter_context(tc.tile_pool(name="sb", bufs=1))
+        mm = ctx.enter_context(tc.psum_pool(name="mm", bufs=3))
+        sums = ctx.enter_context(tc.psum_pool(name="sums", bufs=4))
+
+        def quantize(grouped, name, tags=(None, None)):
+            width = grouped.shape[1] // 4
+            codes = sb.tile([P, width], U32, name=name + "_codes", tag=tags[0] or name + "_codes", align_bytes=64)
+            scales = sb.tile([P, width], U8, name=name + "_scales", tag=tags[1] or name + "_scales", align_bytes=64)
+            nc.vector.quantize_mx(out=codes[:].bitcast(FP8X4), scales=scales[:], in_=grouped)
+            return codes, scales
+
+        def product(acc, lhs, lhs_cols, rhs, start, stop):
+            nc.tensor.matmul_mx(
+                out=acc,
+                lhsT=lhs[0][:, lhs_cols].bitcast(FP8X4),
+                lhsT_scale=lhs[1][:, lhs_cols],
+                rhs=rhs[0][:].bitcast(FP8X4),
+                rhs_scale=rhs[1][:],
+                start=start,
+                stop=stop,
+            )
+
+        def interleave(engine_copy, dst, src):
+            engine_copy(out=dst.rearrange("p (c i) r -> p c r i", i=4), in_=src.rearrange("p r (c i) -> p c r i", i=4))
+
+        offs_sb = lists.tile([P, S // 16], U16, name="offs_sb")
+        nc.sync.dma_start(offs_sb[:], offs)
+        x_rows = xT.rearrange("(p u e) t -> p u e t", u=2, e=2)
+        x_raw = {}
+        for u in range(2):
+            for c in range(T // CHUNK):
+                x_raw[u, c] = sb.tile([P, 2, CHUNK], F32, name=f"x_raw{u}{c}")
+                nc.sync.dma_start(x_raw[u, c][:], x_rows[:, u, :, c * CHUNK : (c + 1) * CHUNK])
+        w1_raw = sb.tile([P, 4, H], F32, name="w1_raw")
+        nc.sync.dma_start(w1_raw[:], w1.rearrange("(p j) c -> p j c", j=4))
+        pos_sb = []
+        for d, pos in enumerate((pos1, pos2, pos3, pos4)):
+            pos_sb.append(lists.tile([P, V // 16], U16, name=f"pos_sb{d}"))
+            nc.sync.dma_start(pos_sb[d][:], pos)
+        w_raw = []
+        for a, w in enumerate((w2, w3, w4)):
+            w_raw.append(sb.tile([P, 4, N], F32, name=f"w_raw{a}"))
+            nc.sync.dma_start(w_raw[a][:], w.rearrange("(p j) c -> p j c", j=4))
+
+        ident = sb.tile([P, P], F32, name="ident")
+        make_identity(nc, ident[:])
+
+        pieces = spans(PIECES)
+        picked = [sb.tile([P, w, 2], U32, name=f"picked{i}", align_bytes=64) for i, w in enumerate(PIECES)]
+        pairs = [sb.tile([P, T], U32, name=f"pairs{u}", align_bytes=64) for u in range(2)]
+        last_chunk = T // CHUNK - 1
+        for u in range(2):
+            for c in range(T // CHUNK):
+                on_scalar = (c == 0) if u == 0 else (c < last_chunk)
+                dst = pairs[u][:, c * CHUNK : (c + 1) * CHUNK].bitcast(BF16).rearrange("p (t e) -> p t e", e=2)
+                interleave(nc.scalar.copy if on_scalar else nc.vector.tensor_copy, dst, x_raw[u, c][:])
+            for i, s in enumerate(pieces):
+                nc.vector.tensor_copy(out=picked[i][:, :, u], in_=pairs[u][:].indirect(offs_sb[:, s.start // 16 : s.stop // 16]))
+
+        w1_grouped = [sb.tile([P, 2, P, 4], BF16, name=f"w1_grouped{u}", align_bytes=64) for u in range(2)]
+        for u in range(2):
+            nc.scalar.copy(
+                out=w1_grouped[u][:].rearrange("p e m j -> p m j e"),
+                in_=w1_raw[:].rearrange("p j (m t) -> p m j t", t=4)[:, :, :, 2 * u : 2 * u + 2],
+            )
+
+        def picked_values(i):
+            return picked[i][:].rearrange("p s u -> p (s u)").bitcast(BF16)
+
+        def w1_values(u):
+            return w1_grouped[u][:].rearrange("p e m j -> p (e m j)")
+
+        x_mx = [quantize(picked_values(0), "x0")]
+        w1_mx = [quantize(w1_values(0), "w1a")]
+        x_mx.append(quantize(picked_values(1), "x1"))
+        x_mx.append(quantize(picked_values(2), "x2", tags=("late1", "late2")))
+        w1_mx.append(quantize(w1_values(1), "w1b", tags=("late3", "late4")))
+
+        h = [sb.tile([P, S], F32, name=f"h{t}") for t in range(4)]
+        for t in range(4):
+            for i, s in enumerate(pieces):
+                acc = mm.tile([P, PIECES[i]], F32, name="acc", tag="bank")
+                product(acc[:], w1_mx[t // 2], slice((t % 2) * P, (t % 2 + 1) * P), x_mx[i], True, True)
+                nc.scalar.copy(out=h[t][:, s], in_=acc[:])
+
+        g = [sb.tile([P, 4, V], F32, name=f"g{d}", tag=f"late{d}", align_bytes=64) for d in range(D)]
+        total = [sums.tile([P, 4, P], F32, name="total") for c in range(V // P)]
+        for d in range(D):
+            for t in range(4):
+                nc.vector.tensor_copy(out=g[d][:, t, :], in_=h[t][:].indirect(pos_sb[d][:]))
+                for c in range(V // P):
+                    nc.tensor.matmul(
+                        out=total[c][:, t, :],
+                        lhsT=g[d][:, t, c * P : (c + 1) * P],
+                        rhs=ident[:],
+                        is_transpose=True,
+                        start=(d == 0 and t == 0),
+                        stop=(d == D - 1 and t == 3),
+                    )
+
+        w_grouped = sb.tile([P, 3, N, 4], BF16, name="w_grouped", tag="late4", align_bytes=64)
+        for a in range(3):
+            interleave(nc.scalar.copy, w_grouped[:, a], w_raw[a][:])
+        w_mx = [quantize(w_grouped[:, a].rearrange("p n j -> p (n j)"), f"w{a}") for a in range(3)]
+
+        rounded = [sb.tile([P, V, 4], BF16, name=f"rounded{d}") for d in range(D)]
+        for d in range(D - 1):
+            interleave(nc.scalar.copy, rounded[d][:], g[d][:])
+
+        parts = spans(PARTS)
+        mean_rows = []
+        for v in parts:
+            interleave(nc.scalar.copy, rounded[D - 1][:, v, :], g[D - 1][:, :, v])
+            for c in range(v.start // P, v.stop // P):
+                mean_rows.append(sb.tile([P, 2, P, 2], BF16, name=f"mean_rows{c}"))
+                nc.scalar.activation(
+                    out=mean_rows[c][:],
+                    in_=total[c][:].rearrange("v (u e) p -> v u p e", u=2),
+                    func=COPY,
+                    scale=1.0 / D,
+                )
+        z1 = []
+        for n, v in enumerate(parts):
+            blocks = PARTS[n] // P
+            back = mm.tile([P, blocks, 2, P], F32, name="back", tag="bank")
+            for b in range(blocks):
+                words = mean_rows[v.start // P + b][:].rearrange("v u p e -> v (u p e)").bitcast(F32)
+                for u in range(2):
+                    nc.tensor.transpose(back[:, b, u, :], words[:, u * P : (u + 1) * P], ident[:])
+            z1.append(sb.tile([P, blocks, P, 2], F32, name=f"z1_{n}", align_bytes=64))
+            nc.scalar.copy(out=z1[n][:], in_=back[:].rearrange("p b u v -> p b v u"))
+
+        def flat(ap):
+            return ap.rearrange("p v t -> p (v t)")
+
+        running = {"hi": rounded[0], "lo": rounded[0]}
+        for d in range(1, D - 1):
+            for op, name in ((MAX, "hi"), (MIN, "lo")):
+                step = sb.tile([P, V, 4], BF16, name=f"{name}{d}")
+                nc.vector.tensor_tensor(out=flat(step[:]), in0=flat(running[name][:]), in1=flat(rounded[d][:]), op=op)
+                running[name] = step
+
+        for n, v in enumerate(parts):
+            z = []
+            for op, name in ((MAX, "hi"), (MIN, "lo")):
+                z.append(sb.tile([P, PARTS[n] * 4], BF16, name=f"z{name}_{n}", align_bytes=64))
+                nc.vector.tensor_tensor(out=z[-1][:], in0=flat(running[name][:, v, :]), in1=flat(rounded[D - 1][:, v, :]), op=op)
+            z_mx = [quantize(z[0][:], f"z2q{n}"), quantize(z[1][:], f"z3q{n}")]
+            z_mx.append(quantize(z1[n][:].rearrange("p b v u -> p (b v u)").bitcast(BF16), f"z1q{n}"))
+            for m in range(N // P):
+                acc = mm.tile([P, PARTS[n]], F32, name="acc", tag="bank")
+                for a, (w, zq) in enumerate(zip((w_mx[1], w_mx[2], w_mx[0]), z_mx)):
+                    product(acc[:], w, slice(m * P, (m + 1) * P), zq, a == 0, a == 2)
+                result = sb.tile([P, PARTS[n]], F32, name=f"result{n}{m}")
+                if n == len(parts) - 1 and m == 1:
+                    nc.vector.tensor_copy(out=result[:], in_=acc[:])
+                else:
+                    nc.scalar.copy(out=result[:], in_=acc[:])
+                nc.sync.dma_start(out[m * P : (m + 1) * P, v], result[:])

@@ -18,9 +18,10 @@ MIN = mybir.AluOpType.min
 
 P = 128
 D = 4
-CHUNK = 512
-PIECES = (512, 256, 256)
-PARTS = (256, 256)
+CHUNKS = ((1024, 512, 512), (512, 512, 512, 384, 128))
+ON_SCALAR = ((0,), (0, 1, 4))
+PIECES = (512, 512)
+PARTS = (256, 128, 128)
 
 
 def spans(widths):
@@ -33,7 +34,7 @@ def tile_picked_pna_none_e_kernel(tc, xT, w1, w2, w3, w4, offs, pos1, pos2, pos3
     with ExitStack() as ctx:
         lists = ctx.enter_context(tc.tile_pool(name="lists", bufs=1))
         sb = ctx.enter_context(tc.tile_pool(name="sb", bufs=1))
-        mm = ctx.enter_context(tc.psum_pool(name="mm", bufs=3))
+        mm = ctx.enter_context(tc.psum_pool(name="mm", bufs=4))
         sums = ctx.enter_context(tc.psum_pool(name="sums", bufs=4))
 
         def quantize(grouped, name, tags=(None, None)):
@@ -43,13 +44,13 @@ def tile_picked_pna_none_e_kernel(tc, xT, w1, w2, w3, w4, offs, pos1, pos2, pos3
             nc.vector.quantize_mx(out=codes[:].bitcast(FP8X4), scales=scales[:], in_=grouped)
             return codes, scales
 
-        def product(acc, lhs, lhs_cols, rhs, start, stop):
+        def product(acc, lhs, lhs_cols, rhs, rhs_cols, start, stop):
             nc.tensor.matmul_mx(
                 out=acc,
                 lhsT=lhs[0][:, lhs_cols].bitcast(FP8X4),
                 lhsT_scale=lhs[1][:, lhs_cols],
-                rhs=rhs[0][:].bitcast(FP8X4),
-                rhs_scale=rhs[1][:],
+                rhs=rhs[0][:, rhs_cols].bitcast(FP8X4),
+                rhs_scale=rhs[1][:, rhs_cols],
                 start=start,
                 stop=stop,
             )
@@ -57,23 +58,26 @@ def tile_picked_pna_none_e_kernel(tc, xT, w1, w2, w3, w4, offs, pos1, pos2, pos3
         def interleave(engine_copy, dst, src):
             engine_copy(out=dst.rearrange("p (c i) r -> p c r i", i=4), in_=src.rearrange("p r (c i) -> p c r i", i=4))
 
-        offs_sb = lists.tile([P, S // 16], U16, name="offs_sb")
-        nc.sync.dma_start(offs_sb[:], offs)
         x_rows = xT.rearrange("(p u e) t -> p u e t", u=2, e=2)
         x_raw = {}
         for u in range(2):
-            for c in range(T // CHUNK):
-                x_raw[u, c] = sb.tile([P, 2, CHUNK], F32, name=f"x_raw{u}{c}")
-                nc.sync.dma_start(x_raw[u, c][:], x_rows[:, u, :, c * CHUNK : (c + 1) * CHUNK])
-        w1_raw = sb.tile([P, 4, H], F32, name="w1_raw")
-        nc.sync.dma_start(w1_raw[:], w1.rearrange("(p j) c -> p j c", j=4))
+            for c, cols in enumerate(spans(CHUNKS[u])):
+                x_raw[u, c] = sb.tile([P, 2, CHUNKS[u][c]], F32, name=f"x_raw{u}{c}")
+                nc.sync.dma_start(x_raw[u, c][:], x_rows[:, u, :, cols])
+            if u == 0:
+                offs_sb = lists.tile([P, S // 16], U16, name="offs_sb")
+                nc.sync.dma_start(offs_sb[:], offs)
+        w1_raw = []
+        for half in range(2):
+            w1_raw.append(sb.tile([P, 4, H // 2], F32, name=f"w1_raw{half}"))
+            nc.sync.dma_start(w1_raw[half][:], w1.rearrange("(p j) (s c) -> p j s c", j=4, s=2)[:, :, half, :])
         pos_sb = []
         for d, pos in enumerate((pos1, pos2, pos3, pos4)):
             pos_sb.append(lists.tile([P, V // 16], U16, name=f"pos_sb{d}"))
             nc.sync.dma_start(pos_sb[d][:], pos)
         w_raw = []
         for a, w in enumerate((w2, w3, w4)):
-            w_raw.append(sb.tile([P, 4, N], F32, name=f"w_raw{a}"))
+            w_raw.append(sb.tile([P, 4, N], F32, name=f"w_raw{a}", align_bytes=64))
             nc.sync.dma_start(w_raw[a][:], w.rearrange("(p j) c -> p j c", j=4))
 
         ident = sb.tile([P, P], F32, name="ident")
@@ -82,42 +86,43 @@ def tile_picked_pna_none_e_kernel(tc, xT, w1, w2, w3, w4, offs, pos1, pos2, pos3
         pieces = spans(PIECES)
         picked = [sb.tile([P, w, 2], U32, name=f"picked{i}", align_bytes=64) for i, w in enumerate(PIECES)]
         pairs = [sb.tile([P, T], U32, name=f"pairs{u}", align_bytes=64) for u in range(2)]
-        last_chunk = T // CHUNK - 1
         for u in range(2):
-            for c in range(T // CHUNK):
-                on_scalar = (c == 0) if u == 0 else (c < last_chunk)
-                dst = pairs[u][:, c * CHUNK : (c + 1) * CHUNK].bitcast(BF16).rearrange("p (t e) -> p t e", e=2)
-                interleave(nc.scalar.copy if on_scalar else nc.vector.tensor_copy, dst, x_raw[u, c][:])
+            for c, cols in enumerate(spans(CHUNKS[u])):
+                dst = pairs[u][:, cols].bitcast(BF16).rearrange("p (t e) -> p t e", e=2)
+                interleave(nc.scalar.copy if c in ON_SCALAR[u] else nc.vector.tensor_copy, dst, x_raw[u, c][:])
             for i, s in enumerate(pieces):
                 nc.vector.tensor_copy(out=picked[i][:, :, u], in_=pairs[u][:].indirect(offs_sb[:, s.start // 16 : s.stop // 16]))
 
-        w1_grouped = [sb.tile([P, 2, P, 4], BF16, name=f"w1_grouped{u}", align_bytes=64) for u in range(2)]
-        for u in range(2):
-            nc.scalar.copy(
-                out=w1_grouped[u][:].rearrange("p e m j -> p m j e"),
-                in_=w1_raw[:].rearrange("p j (m t) -> p m j t", t=4)[:, :, :, 2 * u : 2 * u + 2],
-            )
+        w1_first = sb.tile([P, 1, P, 4], BF16, name="w1_first", tag="late1", align_bytes=64)
+        w1_rest = sb.tile([P, 3, P, 4], BF16, name="w1_rest", align_bytes=64)
+        for half in range(2):
+            src = w1_raw[half][:].rearrange("p j (m t) -> p m j t", t=4)
+            ms = slice(half * P // 2, (half + 1) * P // 2)
+            nc.scalar.copy(out=w1_first[:, :, ms, :].rearrange("p t m j -> p m j t"), in_=src[:, :, :, 0:1])
+            nc.scalar.copy(out=w1_rest[:, :, ms, :].rearrange("p t m j -> p m j t"), in_=src[:, :, :, 1:4])
 
-        def picked_values(i):
-            return picked[i][:].rearrange("p s u -> p (s u)").bitcast(BF16)
+        def w1_values(ap):
+            return ap.rearrange("p t m j -> p (t m j)")
 
-        def w1_values(u):
-            return w1_grouped[u][:].rearrange("p e m j -> p (e m j)")
-
-        x_mx = [quantize(picked_values(0), "x0")]
-        w1_mx = [quantize(w1_values(0), "w1a")]
-        x_mx.append(quantize(picked_values(1), "x1"))
-        x_mx.append(quantize(picked_values(2), "x2", tags=("late1", "late2")))
-        w1_mx.append(quantize(w1_values(1), "w1b", tags=("late3", "late4")))
+        w1_0 = quantize(w1_values(w1_first[:]), "w1_0")
+        x_codes = sb.tile([P, S], U32, name="x_codes", tag="late1", align_bytes=64)
+        x_scales = sb.tile([P, S], U8, name="x_scales", align_bytes=64)
+        quarters = spans((S // 4,) * 4)
+        for q, s in enumerate(quarters):
+            values = picked[q // 2][:, (q % 2) * S // 4 : (q % 2 + 1) * S // 4, :].rearrange("p s u -> p (s u)").bitcast(BF16)
+            nc.vector.quantize_mx(out=x_codes[:, s].bitcast(FP8X4), scales=x_scales[:, s], in_=values)
+        w1_1 = quantize(w1_values(w1_rest[:, 0:1]), "w1_1")
+        w1_23 = quantize(w1_values(w1_rest[:, 1:3]), "w1_23", tags=(None, "late4"))
+        w1_mx = [(w1_0, slice(0, P)), (w1_1, slice(0, P)), (w1_23, slice(0, P)), (w1_23, slice(P, 2 * P))]
 
         h = [sb.tile([P, S], F32, name=f"h{t}") for t in range(4)]
         for t in range(4):
-            for i, s in enumerate(pieces):
-                acc = mm.tile([P, PIECES[i]], F32, name="acc", tag="bank")
-                product(acc[:], w1_mx[t // 2], slice((t % 2) * P, (t % 2 + 1) * P), x_mx[i], True, True)
+            for s in quarters if t == 0 else pieces:
+                acc = mm.tile([P, s.stop - s.start], F32, name="acc", tag="bank")
+                product(acc[:], w1_mx[t][0], w1_mx[t][1], (x_codes, x_scales), s, True, True)
                 nc.scalar.copy(out=h[t][:, s], in_=acc[:])
 
-        g = [sb.tile([P, 4, V], F32, name=f"g{d}", tag=f"late{d}", align_bytes=64) for d in range(D)]
+        g = [sb.tile([P, 4, V], F32, name=f"g{d}", tag=("g0", "g1", "w_raw0", "w_raw1")[d], align_bytes=64) for d in range(D)]
         total = [sums.tile([P, 4, P], F32, name="total") for c in range(V // P)]
         for d in range(D):
             for t in range(4):
@@ -143,7 +148,8 @@ def tile_picked_pna_none_e_kernel(tc, xT, w1, w2, w3, w4, offs, pos1, pos2, pos3
 
         parts = spans(PARTS)
         mean_rows = []
-        for v in parts:
+        z1 = []
+        for n, v in enumerate(parts):
             interleave(nc.scalar.copy, rounded[D - 1][:, v, :], g[D - 1][:, :, v])
             for c in range(v.start // P, v.stop // P):
                 mean_rows.append(sb.tile([P, 2, P, 2], BF16, name=f"mean_rows{c}"))
@@ -153,8 +159,6 @@ def tile_picked_pna_none_e_kernel(tc, xT, w1, w2, w3, w4, offs, pos1, pos2, pos3
                     func=COPY,
                     scale=1.0 / D,
                 )
-        z1 = []
-        for n, v in enumerate(parts):
             blocks = PARTS[n] // P
             back = mm.tile([P, blocks, 2, P], F32, name="back", tag="bank")
             for b in range(blocks):
@@ -167,27 +171,28 @@ def tile_picked_pna_none_e_kernel(tc, xT, w1, w2, w3, w4, offs, pos1, pos2, pos3
         def flat(ap):
             return ap.rearrange("p v t -> p (v t)")
 
-        running = {"hi": rounded[0], "lo": rounded[0]}
-        for d in range(1, D - 1):
-            for op, name in ((MAX, "hi"), (MIN, "lo")):
-                step = sb.tile([P, V, 4], BF16, name=f"{name}{d}")
-                nc.vector.tensor_tensor(out=flat(step[:]), in0=flat(running[name][:]), in1=flat(rounded[d][:]), op=op)
-                running[name] = step
-
         for n, v in enumerate(parts):
+            running = {"hi": flat(rounded[0][:, v, :]), "lo": flat(rounded[0][:, v, :])}
+            for d in range(1, D - 1):
+                for op, name in ((MAX, "hi"), (MIN, "lo")):
+                    step = sb.tile([P, PARTS[n] * 4], BF16, name=f"{name}{d}", tag=f"{name}{(n + d) % 2}")
+                    nc.vector.tensor_tensor(out=step[:], in0=running[name], in1=flat(rounded[d][:, v, :]), op=op)
+                    running[name] = step[:]
             z = []
             for op, name in ((MAX, "hi"), (MIN, "lo")):
                 z.append(sb.tile([P, PARTS[n] * 4], BF16, name=f"z{name}_{n}", align_bytes=64))
-                nc.vector.tensor_tensor(out=z[-1][:], in0=flat(running[name][:, v, :]), in1=flat(rounded[D - 1][:, v, :]), op=op)
-            z_mx = [quantize(z[0][:], f"z2q{n}"), quantize(z[1][:], f"z3q{n}")]
-            z_mx.append(quantize(z1[n][:].rearrange("p b v u -> p (b v u)").bitcast(BF16), f"z1q{n}"))
+                nc.vector.tensor_tensor(out=z[-1][:], in0=running[name], in1=flat(rounded[D - 1][:, v, :]), op=op)
+            values = [z1[n][:].rearrange("p b v u -> p (b v u)").bitcast(BF16), z[0][:], z[1][:]]
+            order = (0, 1, 2) if n == len(parts) - 1 else (1, 2, 0)
+            z_mx = {a: quantize(values[a], f"zq{a}{n}") for a in order}
+            accs = [sums.tile([P, PARTS[n]], F32, name="total") for m in range(N // P)]
+            for a in order:
+                for m in range(N // P):
+                    product(accs[m][:], w_mx[a], slice(m * P, (m + 1) * P), z_mx[a], slice(0, PARTS[n]), a == order[0], a == order[2])
             for m in range(N // P):
-                acc = mm.tile([P, PARTS[n]], F32, name="acc", tag="bank")
-                for a, (w, zq) in enumerate(zip((w_mx[1], w_mx[2], w_mx[0]), z_mx)):
-                    product(acc[:], w, slice(m * P, (m + 1) * P), zq, a == 0, a == 2)
                 result = sb.tile([P, PARTS[n]], F32, name=f"result{n}{m}")
                 if n == len(parts) - 1 and m == 1:
-                    nc.vector.tensor_copy(out=result[:], in_=acc[:])
+                    nc.vector.tensor_copy(out=result[:], in_=accs[m][:])
                 else:
-                    nc.scalar.copy(out=result[:], in_=acc[:])
+                    nc.scalar.copy(out=result[:], in_=accs[m][:])
                 nc.sync.dma_start(out[m * P : (m + 1) * P, v], result[:])

from contextlib import ExitStack

import concourse.mybir as mybir
from concourse.masks import make_identity

K, T, S, V, H, N = 512, 2048, 1024, 512, 512, 256
FLOPS = 2 * (K * H * S + 3 * H * N * V)

F32 = mybir.dt.float32
BF16 = mybir.dt.bfloat16
U32 = mybir.dt.uint32
U16 = mybir.dt.uint16
U8 = mybir.dt.uint8
FP8X4 = mybir.dt.float8_e4m3fn_x4
COPY = mybir.ActivationFunctionType.Copy
MAX = mybir.AluOpType.max
MIN = mybir.AluOpType.min

P = 128
D = 4
CHUNKS = ((1024, 512, 512), (512, 512, 512, 384, 128))
ON_SCALAR = ((0,), (0, 1, 4))
PIECES = (512, 512)
PARTS = (256, 128, 128)


def spans(widths):
    starts = [sum(widths[:i]) for i in range(len(widths))]
    return [slice(a, a + w) for a, w in zip(starts, widths)]


def tile_picked_pna_none_e_kernel(tc, xT, w1, w2, w3, w4, offs, pos1, pos2, pos3, pos4, out):
    nc = tc.nc
    with ExitStack() as ctx:
        lists = ctx.enter_context(tc.tile_pool(name="lists", bufs=1))
        sb = ctx.enter_context(tc.tile_pool(name="sb", bufs=1))
        mm = ctx.enter_context(tc.psum_pool(name="mm", bufs=4))
        sums = ctx.enter_context(tc.psum_pool(name="sums", bufs=4))

        def quantize(grouped, name, tags=(None, None)):
            width = grouped.shape[1] // 4
            codes = sb.tile([P, width], U32, name=name + "_codes", tag=tags[0] or name + "_codes", align_bytes=64)
            scales = sb.tile([P, width], U8, name=name + "_scales", tag=tags[1] or name + "_scales", align_bytes=64)
            nc.vector.quantize_mx(out=codes[:].bitcast(FP8X4), scales=scales[:], in_=grouped)
            return codes, scales

        def product(acc, lhs, lhs_cols, rhs, rhs_cols, start, stop):
            nc.tensor.matmul_mx(
                out=acc,
                lhsT=lhs[0][:, lhs_cols].bitcast(FP8X4),
                lhsT_scale=lhs[1][:, lhs_cols],
                rhs=rhs[0][:, rhs_cols].bitcast(FP8X4),
                rhs_scale=rhs[1][:, rhs_cols],
                start=start,
                stop=stop,
            )

        def interleave(engine_copy, dst, src):
            engine_copy(out=dst.rearrange("p (c i) r -> p c r i", i=4), in_=src.rearrange("p r (c i) -> p c r i", i=4))

        x_rows = xT.rearrange("(p u e) t -> p u e t", u=2, e=2)
        x_raw = {}
        for u in range(2):
            for c, cols in enumerate(spans(CHUNKS[u])):
                x_raw[u, c] = sb.tile([P, 2, CHUNKS[u][c]], F32, name=f"x_raw{u}{c}")
                nc.sync.dma_start(x_raw[u, c][:], x_rows[:, u, :, cols])
            if u == 0:
                offs_sb = lists.tile([P, S // 16], U16, name="offs_sb")
                nc.sync.dma_start(offs_sb[:], offs)
        w1_raw = []
        for half in range(2):
            w1_raw.append(sb.tile([P, 4, H // 2], F32, name=f"w1_raw{half}"))
            nc.sync.dma_start(w1_raw[half][:], w1.rearrange("(p j) (s c) -> p j s c", j=4, s=2)[:, :, half, :])
        pos_sb = []
        for d, pos in enumerate((pos1, pos2, pos3, pos4)):
            pos_sb.append(lists.tile([P, V // 16], U16, name=f"pos_sb{d}"))
            nc.sync.dma_start(pos_sb[d][:], pos)
        w_raw = []
        for a, w in enumerate((w2, w3, w4)):
            w_raw.append(sb.tile([P, 4, N], F32, name=f"w_raw{a}", align_bytes=64))
            nc.sync.dma_start(w_raw[a][:], w.rearrange("(p j) c -> p j c", j=4))

        ident = sb.tile([P, P], F32, name="ident")
        make_identity(nc, ident[:])

        pieces = spans(PIECES)
        picked = [sb.tile([P, w, 2], U32, name=f"picked{i}", align_bytes=64) for i, w in enumerate(PIECES)]
        pairs = [sb.tile([P, T], U32, name=f"pairs{u}", align_bytes=64) for u in range(2)]
        for u in range(2):
            for c, cols in enumerate(spans(CHUNKS[u])):
                dst = pairs[u][:, cols].bitcast(BF16).rearrange("p (t e) -> p t e", e=2)
                interleave(nc.scalar.copy if c in ON_SCALAR[u] else nc.vector.tensor_copy, dst, x_raw[u, c][:])
            for i, s in enumerate(pieces):
                nc.vector.tensor_copy(out=picked[i][:, :, u], in_=pairs[u][:].indirect(offs_sb[:, s.start // 16 : s.stop // 16]))

        w1_first = sb.tile([P, 1, P, 4], BF16, name="w1_first", tag="late1", align_bytes=64)
        w1_rest = sb.tile([P, 3, P, 4], BF16, name="w1_rest", align_bytes=64)
        for half in range(2):
            src = w1_raw[half][:].rearrange("p j (m t) -> p m j t", t=4)
            ms = slice(half * P // 2, (half + 1) * P // 2)
            nc.scalar.copy(out=w1_first[:, :, ms, :].rearrange("p t m j -> p m j t"), in_=src[:, :, :, 0:1])
            nc.scalar.copy(out=w1_rest[:, :, ms, :].rearrange("p t m j -> p m j t"), in_=src[:, :, :, 1:4])

        def w1_values(ap):
            return ap.rearrange("p t m j -> p (t m j)")

        w1_0 = quantize(w1_values(w1_first[:]), "w1_0")
        x_codes = sb.tile([P, S], U32, name="x_codes", tag="late1", align_bytes=64)
        x_scales = sb.tile([P, S], U8, name="x_scales", align_bytes=64)
        quarters = spans((S // 4,) * 4)
        for q, s in enumerate(quarters):
            values = picked[q // 2][:, (q % 2) * S // 4 : (q % 2 + 1) * S // 4, :].rearrange("p s u -> p (s u)").bitcast(BF16)
            nc.vector.quantize_mx(out=x_codes[:, s].bitcast(FP8X4), scales=x_scales[:, s], in_=values)
        w1_1 = quantize(w1_values(w1_rest[:, 0:1]), "w1_1")
        w1_23 = quantize(w1_values(w1_rest[:, 1:3]), "w1_23", tags=(None, "late4"))
        w1_mx = [(w1_0, slice(0, P)), (w1_1, slice(0, P)), (w1_23, slice(0, P)), (w1_23, slice(P, 2 * P))]

        h = [sb.tile([P, S], F32, name=f"h{t}") for t in range(4)]
        for t in range(4):
            for s in quarters if t == 0 else pieces:
                acc = mm.tile([P, s.stop - s.start], F32, name="acc", tag="bank")
                product(acc[:], w1_mx[t][0], w1_mx[t][1], (x_codes, x_scales), s, True, True)
                nc.scalar.copy(out=h[t][:, s], in_=acc[:])

        g = [sb.tile([P, 4, V], F32, name=f"g{d}", tag=("g0", "g1", "w_raw0", "w_raw1")[d], align_bytes=64) for d in range(D)]
        total = [sums.tile([P, 4, P], F32, name="total") for c in range(V // P)]
        for d in range(D):
            for t in range(4):
                nc.vector.tensor_copy(out=g[d][:, t, :], in_=h[t][:].indirect(pos_sb[d][:]))
                for c in range(V // P):
                    nc.tensor.matmul(
                        out=total[c][:, t, :],
                        lhsT=g[d][:, t, c * P : (c + 1) * P],
                        rhs=ident[:],
                        is_transpose=True,
                        start=(d == 0 and t == 0),
                        stop=(d == D - 1 and t == 3),
                    )

        w_grouped = sb.tile([P, 3, N, 4], BF16, name="w_grouped", tag="late4", align_bytes=64)
        for a in range(3):
            interleave(nc.scalar.copy, w_grouped[:, a], w_raw[a][:])
        w_mx = [quantize(w_grouped[:, a].rearrange("p n j -> p (n j)"), f"w{a}") for a in range(3)]

        rounded = [sb.tile([P, V, 4], BF16, name=f"rounded{d}") for d in range(D)]
        for d in range(D - 1):
            interleave(nc.scalar.copy, rounded[d][:], g[d][:])

        parts = spans(PARTS)
        mean_rows = []
        z1 = []
        for n, v in enumerate(parts):
            interleave(nc.scalar.copy, rounded[D - 1][:, v, :], g[D - 1][:, :, v])
            for c in range(v.start // P, v.stop // P):
                mean_rows.append(sb.tile([P, 2, P, 2], BF16, name=f"mean_rows{c}"))
                nc.scalar.activation(
                    out=mean_rows[c][:],
                    in_=total[c][:].rearrange("v (u e) p -> v u p e", u=2),
                    func=COPY,
                    scale=1.0 / D,
                )
            blocks = PARTS[n] // P
            back = mm.tile([P, blocks, 2, P], F32, name="back", tag="bank")
            for b in range(blocks):
                words = mean_rows[v.start // P + b][:].rearrange("v u p e -> v (u p e)").bitcast(F32)
                for u in range(2):
                    nc.tensor.transpose(back[:, b, u, :], words[:, u * P : (u + 1) * P], ident[:])
            z1.append(sb.tile([P, blocks, P, 2], F32, name=f"z1_{n}", align_bytes=64))
            nc.scalar.copy(out=z1[n][:], in_=back[:].rearrange("p b u v -> p b v u"))

        def flat(ap):
            return ap.rearrange("p v t -> p (v t)")

        for n, v in enumerate(parts):
            running = {"hi": flat(rounded[0][:, v, :]), "lo": flat(rounded[0][:, v, :])}
            for d in range(1, D - 1):
                for op, name in ((MAX, "hi"), (MIN, "lo")):
                    step = sb.tile([P, PARTS[n] * 4], BF16, name=f"{name}{d}", tag=f"{name}{(n + d) % 2}")
                    nc.vector.tensor_tensor(out=step[:], in0=running[name], in1=flat(rounded[d][:, v, :]), op=op)
                    running[name] = step[:]
            z = []
            for op, name in ((MAX, "hi"), (MIN, "lo")):
                z.append(sb.tile([P, PARTS[n] * 4], BF16, name=f"z{name}_{n}", align_bytes=64))
                nc.vector.tensor_tensor(out=z[-1][:], in0=running[name], in1=flat(rounded[D - 1][:, v, :]), op=op)
            values = [z1[n][:].rearrange("p b v u -> p (b v u)").bitcast(BF16), z[0][:], z[1][:]]
            order = (0, 1, 2) if n == len(parts) - 1 else (1, 2, 0)
            z_mx = {a: quantize(values[a], f"zq{a}{n}") for a in order}
            accs = [sums.tile([P, PARTS[n]], F32, name="total") for m in range(N // P)]
            for a in order:
                for m in range(N // P):
                    product(accs[m][:], w_mx[a], slice(m * P, (m + 1) * P), z_mx[a], slice(0, PARTS[n]), a == order[0], a == order[2])
            for m in range(N // P):
                result = sb.tile([P, PARTS[n]], F32, name=f"result{n}{m}")
                if n == len(parts) - 1 and m == 1:
                    nc.vector.tensor_copy(out=result[:], in_=accs[m][:])
                else:
                    nc.scalar.copy(out=result[:], in_=accs[m][:])
                nc.sync.dma_start(out[m * P : (m + 1) * P, v], result[:])
